import numpy as np, ml_dtypes
CORES = [22,38,54,62,70,110,23,39,55,63,71,111]
N = 12
DEG, TK = 4, 128
MASK = [[0,2,3,1],[0,2,3,1],[0,2,3,1],[0,2,3,1],[0,2,3,4],[0,2,3,5],[0,2,3,6],[0,2,3,7],[0,2,3,8],[0,2,3,9],[0,2,3,10],[0,2,3,11]]
def setup_inputs(rng):
    return {"x": rng.standard_normal((N, 128, TK), dtype=np.float32).astype(ml_dtypes.bfloat16), "w": rng.standard_normal((N, 128, DEG * 128), dtype=np.float32).astype(ml_dtypes.bfloat16)}
def setup_inputs_big(rng):
    d = setup_inputs(rng)
    for k in ("x", "w"): d[k] = (d[k].astype(np.float32) * 1024.0).astype(d[k].dtype)
    return d
def setup_inputs_small(rng):
    d = setup_inputs(rng)
    for k in ("x", "w"): d[k] = (d[k].astype(np.float32) * (1 / 1024.0)).astype(d[k].dtype)
    return d
def setup_inputs_apart(rng):
    d = setup_inputs(rng)
    f = (10.0 ** rng.permutation(np.linspace(-1.5, 1.5, N))).astype(np.float32).reshape(N, 1, 1)
    for k in ("x", "w"): d[k] = (d[k].astype(np.float32) * f).astype(d[k].dtype)
    return d
def reference(x, w):
    X, W = x.astype(np.float64), w.astype(np.float64)
    y = np.zeros((N, 128, TK))
    for r in range(N):
        for i, j in enumerate(MASK[r]):
            y[r] += W[r][:, 128 * i:128 * i + 128].T @ X[j]
    return {"y": y.astype(ml_dtypes.bfloat16 if x.dtype != np.float64 else np.float64)}

@@ -1,0 +1,240 @@
+from concourse.bass import DstId, RemoteDMATransfer
+
+TK = 128
+DEG = 4
+POLICY = "warm"
+
+SCRATCH = {
+    "xd": ("dram", [128, TK], "bfloat16"),
+    "land": ("dram", [DEG, 128, TK], "bfloat16"),
+    "xin": ("sbuf", [128, DEG * TK], "bfloat16"),
+    "ws": ("sbuf", [128, DEG * 128], "bfloat16"),
+    "ys": ("sbuf", [128, TK], "bfloat16"),
+    "acc": ("psum", [128, TK], "float32"),
+}
+SEMAPHORES = (["staged", "wl", "own", "sent", "mm", "cp", "stored"]
+              + ["arr%d" % i for i in range(DEG)] + ["ld%d" % i for i in range(DEG)])
+
+
+def _bits(m):
+    return bin(m).count("1")
+
+
+def _order(far, cores, topo, senders):
+    js = sorted(far)
+    turns = max(len(far[j]) for j in js)
+
+    def chip_of(w):
+        return topo.chip(cores[w[0]])
+
+    def key(w):
+        return 0 if (w[1] and w[0] not in senders) else (1 if w[1] else 2)
+
+    left = {j: sorted(far[j], key=key) for j in js}
+    out = {j: [] for j in js}
+
+    def feasible(t):
+        inb = {}
+        for j in js:
+            for w in left[j]:
+                inb[chip_of(w)] = inb.get(chip_of(w), 0) + 1
+        return all(v <= turns - t for v in inb.values())
+
+    def go(t, k, used):
+        if k == len(js):
+            if not any(left[j] for j in js):
+                return True
+            return feasible(t + 1) and go(t + 1, 0, ())
+        j = js[k]
+        if not left[j]:
+            return go(t, k + 1, used)
+        seen = []
+        for w in list(left[j]):
+            c = chip_of(w)
+            if c in used or (c, key(w)) in seen:
+                continue
+            seen.append((c, key(w)))
+            left[j].remove(w)
+            out[j].append(w)
+            if go(t, k + 1, used + (c,)):
+                return True
+            out[j].pop()
+            left[j].append(w)
+            left[j].sort(key=key)
+        return False
+
+    if go(0, 0, ()):
+        return out
+    return {j: sorted(far[j], key=key) for j in js}
+
+
+def make_plan(cores, mask_tbl, topo, policy):
+    cons = {}
+    for r, row in enumerate(mask_tbl):
+        for j in row:
+            if j != r:
+                cons.setdefault(j, []).append(r)
+    senders = set(cons)
+    far, near = {}, {}
+    for j in sorted(cons):
+        groups = {}
+        for r in cons[j]:
+            groups.setdefault(topo.chip(cores[r]), []).append(r)
+        far[j], near[j] = [], []
+        for ch in sorted(groups):
+            rs = groups[ch]
+            if ch == topo.chip(cores[j]):
+                near[j] = rs
+                continue
+            heads = [r for r in rs if policy == "all" or (policy == "warm" and r in senders)]
+            if len(rs) > 1 and heads:
+                far[j].append((heads[0], tuple(r for r in rs if r != heads[0])))
+            else:
+                far[j].extend((r, ()) for r in rs)
+    far = _order(far, cores, topo, senders)
+    due = [[None] * len(row) for row in mask_tbl]
+    for r, row in enumerate(mask_tbl):
+        for i, j in enumerate(row):
+            if j == r:
+                due[r][i] = ("own", 0.0)
+            elif r in near[j]:
+                due[r][i] = ("sbuf", 0.5)
+            else:
+                for t, (h, rest) in enumerate(far[j]):
+                    if h == r:
+                        due[r][i] = ("dram", t + 1.0)
+                    elif r in rest:
+                        due[r][i] = ("sbuf", t + 2.5)
+    return far, near, due
+
+
+def rank_program(g, core, T, topo):
+    rank = T.rank_of(core)
+    if rank is None:
+        return
+    cores = list(T.cores)
+    mask_tbl = T.tables["MASK"]
+    far, near, due = make_plan(cores, mask_tbl, topo, POLICY)
+    row = mask_tbl[rank]
+    sem = T.sem
+
+    def slot_of(r, j):
+        return mask_tbl[r].index(j)
+
+    def sb(i):
+        return T.xin[:, i * TK:(i + 1) * TK]
+
+    every = 0
+    for c in cores:
+        if c != core:
+            every = topo.mask(core, c) if every == 0 else (every & topo.mask(core, c))
+
+    def chip_mask(dst):
+        m = topo.mask(core, dst) & ~every
+        return m if m else topo.mask(core, dst)
+
+    def inc_of(src_core, dst_core, on_chip):
+        ev = 0
+        for c in cores:
+            if c != src_core:
+                ev = topo.mask(src_core, c) if ev == 0 else (ev & topo.mask(src_core, c))
+        if not on_chip:
+            return _bits(ev)
+        m = topo.mask(src_core, dst_core) & ~ev
+        return _bits(m if m else topo.mask(src_core, dst_core))
+
+    sent = [0]
+
+    def send(src_ap, dsts, mask, rsem):
+        ids = []
+        for c, _ap in dsts:
+            assert topo.may_write(core, c)
+            rid, pid, _se = topo.addr(c)
+            ids.append(DstId(rid=rid, pnc=pid))
+        g.remote_dma_fused([RemoteDMATransfer(dst_ids=ids, dma_engine_mask=mask, remote_sem=rsem, srcs=[src_ap],
+                                              dsts=[ap for _c, ap in dsts], alu_op=0)], local_sem=sem.sent)
+        sent[0] += _bits(mask)
+
+    owner = rank in far
+
+    own_slot = row.index(rank) if rank in row else None
+    if owner:
+        g.sync.dma_start(T.xd[:], T.x[:]).then_inc(sem.staged, 16)
+        g.sync.dma_start(T.ws[:], T.w[:]).then_inc(sem.wl, 16)
+        if own_slot is not None:
+            g.sync.dma_start(sb(own_slot), T.x[:]).then_inc(sem.own, 16)
+    else:
+        g.sync.dma_start(T.ws[:], T.w[:]).then_inc(sem.wl, 16)
+        if own_slot is not None:
+            g.scalar.dma_start(sb(own_slot), T.x[:]).then_inc(sem.own, 16)
+
+    if owner:
+        g.wait_ge(sem.staged, 16)
+        for group, landing in ((far[rank], "dram"), ([(r, ()) for r in near[rank]], "sbuf")):
+            by_slot = {}
+            for h, _rest in group:
+                by_slot.setdefault(slot_of(h, rank), []).append(h)
+            for i in sorted(by_slot):
+                hs = by_slot[i]
+                if landing == "dram":
+                    send(T.xd[:], [(cores[h], T.land[i]) for h in hs], every, sem["arr%d" % i])
+                else:
+                    m = chip_mask(cores[hs[0]])
+                    send(T.xd[:], [(cores[h], sb(i)) for h in hs], m, sem["arr%d" % i])
+
+    order = sorted(range(len(row)), key=lambda i: due[rank][i][1])
+    need = {}
+    for i in order:
+        j = row[i]
+        kind = due[rank][i][0]
+        if kind == "dram":
+            need[i] = inc_of(cores[j], core, False)
+        elif kind == "sbuf":
+            if rank in near[j]:
+                need[i] = inc_of(cores[j], core, True)
+            else:
+                h = [h for h, rest in far[j] if rank in rest][0]
+                need[i] = inc_of(cores[h], core, True)
+
+    queues = [g.scalar, g.sync]
+    k = 0
+    for i in order:
+        if due[rank][i][0] != "dram":
+            continue
+        j = row[i]
+        q = queues[k % 2]
+        k += 1
+        q.wait_ge(sem["arr%d" % i], need[i])
+        q.dma_start(sb(i), T.land[i]).then_inc(sem["ld%d" % i], 16)
+        rest = [rest for h, rest in far[j] if h == rank][0]
+        if rest:
+            by_slot = {}
+            for r in rest:
+                by_slot.setdefault(slot_of(r, j), []).append(r)
+            g.wait_ge(sem["arr%d" % i], need[i])
+            for i2 in sorted(by_slot):
+                rs = by_slot[i2]
+                send(T.land[i], [(cores[r], sb(i2)) for r in rs], chip_mask(cores[rs[0]]), sem["arr%d" % i2])
+
+    g.tensor.wait_ge(sem.wl, 16)
+    for n, i in enumerate(order):
+        kind = due[rank][i][0]
+        if kind == "own":
+            g.tensor.wait_ge(sem.own, 16)
+        elif kind == "dram":
+            g.tensor.wait_ge(sem["ld%d" % i], 16)
+        else:
+            g.tensor.wait_ge(sem["arr%d" % i], need[i])
+        mm = g.tensor.matmul(T.acc[:], T.ws[:, i * 128:(i + 1) * 128], sb(i), start=(n == 0),
+                             stop=(n == len(order) - 1))
+        if n == len(order) - 1:
+            mm.then_inc(sem.mm, 1)
+
+    g.vector.wait_ge(sem.mm, 1)
+    g.vector.tensor_copy(T.ys[:], T.acc[:]).then_inc(sem.cp, 1)
+    g.sync.wait_ge(sem.cp, 1)
+    g.sync.dma_start(T.y[:], T.ys[:]).then_inc(sem.stored, 16)
+
+    if sent[0]:
+        g.wait_ge(sem.sent, sent[0])
+    g.wait_ge(sem.stored, 16)

@@ -2,7 +2,6 @@ from concourse.bass import DstId, RemoteDMATransfer
 
 TK = 128
 DEG = 4
-POLICY = "warm"
 
 SCRATCH = {
     "xd": ("dram", [128, TK], "bfloat16"),
@@ -20,55 +19,24 @@ def _bits(m):
     return bin(m).count("1")
 
 
-def _order(far, cores, topo, senders):
-    js = sorted(far)
-    turns = max(len(far[j]) for j in js)
-
-    def chip_of(w):
-        return topo.chip(cores[w[0]])
-
-    def key(w):
-        return 0 if (w[1] and w[0] not in senders) else (1 if w[1] else 2)
-
-    left = {j: sorted(far[j], key=key) for j in js}
-    out = {j: [] for j in js}
-
-    def feasible(t):
-        inb = {}
-        for j in js:
-            for w in left[j]:
-                inb[chip_of(w)] = inb.get(chip_of(w), 0) + 1
-        return all(v <= turns - t for v in inb.values())
-
-    def go(t, k, used):
-        if k == len(js):
-            if not any(left[j] for j in js):
-                return True
-            return feasible(t + 1) and go(t + 1, 0, ())
-        j = js[k]
-        if not left[j]:
-            return go(t, k + 1, used)
-        seen = []
-        for w in list(left[j]):
-            c = chip_of(w)
-            if c in used or (c, key(w)) in seen:
-                continue
-            seen.append((c, key(w)))
-            left[j].remove(w)
-            out[j].append(w)
-            if go(t, k + 1, used + (c,)):
-                return True
-            out[j].pop()
-            left[j].append(w)
-            left[j].sort(key=key)
-        return False
-
-    if go(0, 0, ()):
-        return out
-    return {j: sorted(far[j], key=key) for j in js}
+def far_mask(cores, topo, src):
+    m = 0
+    for c in cores:
+        if c != src:
+            m = topo.mask(src, c) if m == 0 else (m & topo.mask(src, c))
+    return m
 
 
-def make_plan(cores, mask_tbl, topo, policy):
+def near_mask(cores, topo, src, dst):
+    m = topo.mask(src, dst) & ~far_mask(cores, topo, src)
+    return m if m else topo.mask(src, dst)
+
+
+def pass_mask(cores, topo, src, dst):
+    return topo.mask(src, dst)
+
+
+def make_plan(cores, mask_tbl, topo):
     cons = {}
     for r, row in enumerate(mask_tbl):
         for j in row:
@@ -80,31 +48,56 @@ def make_plan(cores, mask_tbl, topo, policy):
         groups = {}
         for r in cons[j]:
             groups.setdefault(topo.chip(cores[r]), []).append(r)
-        far[j], near[j] = [], []
+        near[j] = groups.pop(topo.chip(cores[j]), [])
+        far[j] = []
         for ch in sorted(groups):
             rs = groups[ch]
-            if ch == topo.chip(cores[j]):
-                near[j] = rs
-                continue
-            heads = [r for r in rs if policy == "all" or (policy == "warm" and r in senders)]
-            if len(rs) > 1 and heads:
-                far[j].append((heads[0], tuple(r for r in rs if r != heads[0])))
-            else:
-                far[j].extend((r, ()) for r in rs)
-    far = _order(far, cores, topo, senders)
+            h = ([r for r in rs if r in senders] + rs)[0]
+            far[j].append((h, tuple(r for r in rs if r != h)))
+
+    keys = sorted(far, key=lambda j: (-len(cons[j]), j))
+    left = {j: list(far[j]) for j in keys}
+    far = {j: [] for j in keys}
+
+    def first(w):
+        return 0 if (w[1] and w[0] not in senders) else (1 if w[1] else 2)
+
+    while any(left.values()):
+        used = []
+        for j in keys:
+            if left[j]:
+                free = [w for w in left[j] if topo.chip(cores[w[0]]) not in used] or left[j]
+                w = min(free, key=lambda w: (first(w), -sum(topo.chip(cores[v[0]]) == topo.chip(cores[w[0]])
+                                                            for o in keys for v in left[o])))
+                left[j].remove(w)
+                far[j].append(w)
+                used.append(topo.chip(cores[w[0]]))
+
+    lone = {}
+    for j in far:
+        for t, (h, rest) in enumerate(far[j]):
+            if rest and h not in senders:
+                lone.setdefault(topo.chip(cores[h]), []).append((t, j))
+    for ch in lone:
+        for n, (t, j) in enumerate(sorted(lone[ch])):
+            h, rest = far[j][t]
+            rs = sorted((h,) + rest)
+            h = rs[n % len(rs)]
+            far[j][t] = (h, tuple(r for r in rs if r != h))
+
     due = [[None] * len(row) for row in mask_tbl]
     for r, row in enumerate(mask_tbl):
         for i, j in enumerate(row):
             if j == r:
-                due[r][i] = ("own", 0.0)
+                due[r][i] = ("own", 0.0, 0)
             elif r in near[j]:
-                due[r][i] = ("sbuf", 0.5)
+                due[r][i] = ("sbuf", 0.5, _bits(near_mask(cores, topo, cores[j], cores[r])))
             else:
                 for t, (h, rest) in enumerate(far[j]):
                     if h == r:
-                        due[r][i] = ("dram", t + 1.0)
+                        due[r][i] = ("dram", t + 1.0, _bits(far_mask(cores, topo, cores[j])))
                     elif r in rest:
-                        due[r][i] = ("sbuf", t + 2.5)
+                        due[r][i] = ("sbuf", t + 3.5, _bits(pass_mask(cores, topo, cores[h], cores[r])))
     return far, near, due
 
 
@@ -114,7 +107,7 @@ def rank_program(g, core, T, topo):
         return
     cores = list(T.cores)
     mask_tbl = T.tables["MASK"]
-    far, near, due = make_plan(cores, mask_tbl, topo, POLICY)
+    far, near, due = make_plan(cores, mask_tbl, topo)
     row = mask_tbl[rank]
     sem = T.sem
 
@@ -123,25 +116,6 @@ def rank_program(g, core, T, topo):
 
     def sb(i):
         return T.xin[:, i * TK:(i + 1) * TK]
-
-    every = 0
-    for c in cores:
-        if c != core:
-            every = topo.mask(core, c) if every == 0 else (every & topo.mask(core, c))
-
-    def chip_mask(dst):
-        m = topo.mask(core, dst) & ~every
-        return m if m else topo.mask(core, dst)
-
-    def inc_of(src_core, dst_core, on_chip):
-        ev = 0
-        for c in cores:
-            if c != src_core:
-                ev = topo.mask(src_core, c) if ev == 0 else (ev & topo.mask(src_core, c))
-        if not on_chip:
-            return _bits(ev)
-        m = topo.mask(src_core, dst_core) & ~ev
-        return _bits(m if m else topo.mask(src_core, dst_core))
 
     sent = [0]
 
@@ -170,61 +144,42 @@ def rank_program(g, core, T, topo):
 
     if owner:
         g.wait_ge(sem.staged, 16)
-        for group, landing in ((far[rank], "dram"), ([(r, ()) for r in near[rank]], "sbuf")):
-            by_slot = {}
-            for h, _rest in group:
-                by_slot.setdefault(slot_of(h, rank), []).append(h)
-            for i in sorted(by_slot):
-                hs = by_slot[i]
-                if landing == "dram":
-                    send(T.xd[:], [(cores[h], T.land[i]) for h in hs], every, sem["arr%d" % i])
-                else:
-                    m = chip_mask(cores[hs[0]])
-                    send(T.xd[:], [(cores[h], sb(i)) for h in hs], m, sem["arr%d" % i])
+        slots = set(slot_of(r, rank) for r in range(len(cores)) if r != rank and rank in mask_tbl[r])
+        assert len(slots) == 1
+        i = slots.pop()
+        send(T.xd[:], [(cores[h], T.land[i]) for h, _rest in far[rank]], far_mask(cores, topo, core),
+             sem["arr%d" % i])
+        if near[rank]:
+            send(T.xd[:], [(cores[r], sb(i)) for r in near[rank]], near_mask(cores, topo, core, cores[near[rank][0]]),
+                 sem["arr%d" % i])
 
     order = sorted(range(len(row)), key=lambda i: due[rank][i][1])
-    need = {}
-    for i in order:
-        j = row[i]
-        kind = due[rank][i][0]
-        if kind == "dram":
-            need[i] = inc_of(cores[j], core, False)
-        elif kind == "sbuf":
-            if rank in near[j]:
-                need[i] = inc_of(cores[j], core, True)
-            else:
-                h = [h for h, rest in far[j] if rank in rest][0]
-                need[i] = inc_of(cores[h], core, True)
-
     queues = [g.scalar, g.sync]
     k = 0
     for i in order:
-        if due[rank][i][0] != "dram":
+        where, _turn, inc = due[rank][i]
+        if where != "dram":
             continue
         j = row[i]
         q = queues[k % 2]
         k += 1
-        q.wait_ge(sem["arr%d" % i], need[i])
+        q.wait_ge(sem["arr%d" % i], inc)
         q.dma_start(sb(i), T.land[i]).then_inc(sem["ld%d" % i], 16)
-        rest = [rest for h, rest in far[j] if h == rank][0]
+        rest = [w[1] for w in far[j] if w[0] == rank][0]
         if rest:
-            by_slot = {}
-            for r in rest:
-                by_slot.setdefault(slot_of(r, j), []).append(r)
-            g.wait_ge(sem["arr%d" % i], need[i])
-            for i2 in sorted(by_slot):
-                rs = by_slot[i2]
-                send(T.land[i], [(cores[r], sb(i2)) for r in rs], chip_mask(cores[rs[0]]), sem["arr%d" % i2])
+            g.wait_ge(sem["arr%d" % i], inc)
+            send(T.land[i], [(cores[r], sb(slot_of(r, j))) for r in rest],
+                 pass_mask(cores, topo, core, cores[rest[0]]), sem["arr%d" % i])
 
     g.tensor.wait_ge(sem.wl, 16)
     for n, i in enumerate(order):
-        kind = due[rank][i][0]
-        if kind == "own":
+        where, _turn, inc = due[rank][i]
+        if where == "own":
             g.tensor.wait_ge(sem.own, 16)
-        elif kind == "dram":
+        elif where == "dram":
             g.tensor.wait_ge(sem["ld%d" % i], 16)
         else:
-            g.tensor.wait_ge(sem["arr%d" % i], need[i])
+            g.tensor.wait_ge(sem["arr%d" % i], inc)
         mm = g.tensor.matmul(T.acc[:], T.ws[:, i * 128:(i + 1) * 128], sb(i), start=(n == 0),
                              stop=(n == len(order) - 1))
         if n == len(order) - 1:

from concourse.bass import DstId, RemoteDMATransfer

TK = 128
DEG = 4

SCRATCH = {
    "xd": ("dram", [128, TK], "bfloat16"),
    "land": ("dram", [DEG, 128, TK], "bfloat16"),
    "xin": ("sbuf", [128, DEG * TK], "bfloat16"),
    "ws": ("sbuf", [128, DEG * 128], "bfloat16"),
    "ys": ("sbuf", [128, TK], "bfloat16"),
    "acc": ("psum", [128, TK], "float32"),
}
SEMAPHORES = (["staged", "wl", "own", "sent", "mm", "cp", "stored"]
              + ["arr%d" % i for i in range(DEG)] + ["ld%d" % i for i in range(DEG)])


def _bits(m):
    return bin(m).count("1")


def far_mask(cores, topo, src):
    m = 0
    for c in cores:
        if c != src:
            m = topo.mask(src, c) if m == 0 else (m & topo.mask(src, c))
    return m


def near_mask(cores, topo, src, dst):
    m = topo.mask(src, dst) & ~far_mask(cores, topo, src)
    return m if m else topo.mask(src, dst)


def pass_mask(cores, topo, src, dst):
    return topo.mask(src, dst)


def make_plan(cores, mask_tbl, topo):
    cons = {}
    for r, row in enumerate(mask_tbl):
        for j in row:
            if j != r:
                cons.setdefault(j, []).append(r)
    senders = set(cons)
    far, near = {}, {}
    for j in sorted(cons):
        groups = {}
        for r in cons[j]:
            groups.setdefault(topo.chip(cores[r]), []).append(r)
        near[j] = groups.pop(topo.chip(cores[j]), [])
        far[j] = []
        for ch in sorted(groups):
            rs = groups[ch]
            h = ([r for r in rs if r in senders] + rs)[0]
            far[j].append((h, tuple(r for r in rs if r != h)))

    keys = sorted(far, key=lambda j: (-len(cons[j]), j))
    left = {j: list(far[j]) for j in keys}
    far = {j: [] for j in keys}

    def first(w):
        return 0 if (w[1] and w[0] not in senders) else (1 if w[1] else 2)

    while any(left.values()):
        used = []
        for j in keys:
            if left[j]:
                free = [w for w in left[j] if topo.chip(cores[w[0]]) not in used] or left[j]
                w = min(free, key=lambda w: (first(w), -sum(topo.chip(cores[v[0]]) == topo.chip(cores[w[0]])
                                                            for o in keys for v in left[o])))
                left[j].remove(w)
                far[j].append(w)
                used.append(topo.chip(cores[w[0]]))

    lone = {}
    for j in far:
        for t, (h, rest) in enumerate(far[j]):
            if rest and h not in senders:
                lone.setdefault(topo.chip(cores[h]), []).append((t, j))
    for ch in lone:
        for n, (t, j) in enumerate(sorted(lone[ch])):
            h, rest = far[j][t]
            rs = sorted((h,) + rest)
            h = rs[n % len(rs)]
            far[j][t] = (h, tuple(r for r in rs if r != h))

    due = [[None] * len(row) for row in mask_tbl]
    for r, row in enumerate(mask_tbl):
        for i, j in enumerate(row):
            if j == r:
                due[r][i] = ("own", 0.0, 0)
            elif r in near[j]:
                due[r][i] = ("sbuf", 0.5, _bits(near_mask(cores, topo, cores[j], cores[r])))
            else:
                for t, (h, rest) in enumerate(far[j]):
                    if h == r:
                        due[r][i] = ("dram", t + 1.0, _bits(far_mask(cores, topo, cores[j])))
                    elif r in rest:
                        due[r][i] = ("sbuf", t + 3.5, _bits(pass_mask(cores, topo, cores[h], cores[r])))
    return far, near, due


def rank_program(g, core, T, topo):
    rank = T.rank_of(core)
    if rank is None:
        return
    cores = list(T.cores)
    mask_tbl = T.tables["MASK"]
    far, near, due = make_plan(cores, mask_tbl, topo)
    row = mask_tbl[rank]
    sem = T.sem

    def slot_of(r, j):
        return mask_tbl[r].index(j)

    def sb(i):
        return T.xin[:, i * TK:(i + 1) * TK]

    sent = [0]

    def send(src_ap, dsts, mask, rsem):
        ids = []
        for c, _ap in dsts:
            assert topo.may_write(core, c)
            rid, pid, _se = topo.addr(c)
            ids.append(DstId(rid=rid, pnc=pid))
        g.remote_dma_fused([RemoteDMATransfer(dst_ids=ids, dma_engine_mask=mask, remote_sem=rsem, srcs=[src_ap],
                                              dsts=[ap for _c, ap in dsts], alu_op=0)], local_sem=sem.sent)
        sent[0] += _bits(mask)

    owner = rank in far

    own_slot = row.index(rank) if rank in row else None
    if owner:
        g.sync.dma_start(T.xd[:], T.x[:]).then_inc(sem.staged, 16)
        g.sync.dma_start(T.ws[:], T.w[:]).then_inc(sem.wl, 16)
        if own_slot is not None:
            g.sync.dma_start(sb(own_slot), T.x[:]).then_inc(sem.own, 16)
    else:
        g.sync.dma_start(T.ws[:], T.w[:]).then_inc(sem.wl, 16)
        if own_slot is not None:
            g.scalar.dma_start(sb(own_slot), T.x[:]).then_inc(sem.own, 16)

    if owner:
        g.wait_ge(sem.staged, 16)
        slots = set(slot_of(r, rank) for r in range(len(cores)) if r != rank and rank in mask_tbl[r])
        assert len(slots) == 1
        i = slots.pop()
        send(T.xd[:], [(cores[h], T.land[i]) for h, _rest in far[rank]], far_mask(cores, topo, core),
             sem["arr%d" % i])
        if near[rank]:
            send(T.xd[:], [(cores[r], sb(i)) for r in near[rank]], near_mask(cores, topo, core, cores[near[rank][0]]),
                 sem["arr%d" % i])

    order = sorted(range(len(row)), key=lambda i: due[rank][i][1])
    queues = [g.scalar, g.sync]
    k = 0
    for i in order:
        where, _turn, inc = due[rank][i]
        if where != "dram":
            continue
        j = row[i]
        q = queues[k % 2]
        k += 1
        q.wait_ge(sem["arr%d" % i], inc)
        q.dma_start(sb(i), T.land[i]).then_inc(sem["ld%d" % i], 16)
        rest = [w[1] for w in far[j] if w[0] == rank][0]
        if rest:
            g.wait_ge(sem["arr%d" % i], inc)
            send(T.land[i], [(cores[r], sb(slot_of(r, j))) for r in rest],
                 pass_mask(cores, topo, core, cores[rest[0]]), sem["arr%d" % i])

    g.tensor.wait_ge(sem.wl, 16)
    for n, i in enumerate(order):
        where, _turn, inc = due[rank][i]
        if where == "own":
            g.tensor.wait_ge(sem.own, 16)
        elif where == "dram":
            g.tensor.wait_ge(sem["ld%d" % i], 16)
        else:
            g.tensor.wait_ge(sem["arr%d" % i], inc)
        mm = g.tensor.matmul(T.acc[:], T.ws[:, i * 128:(i + 1) * 128], sb(i), start=(n == 0),
                             stop=(n == len(order) - 1))
        if n == len(order) - 1:
            mm.then_inc(sem.mm, 1)

    g.vector.wait_ge(sem.mm, 1)
    g.vector.tensor_copy(T.ys[:], T.acc[:]).then_inc(sem.cp, 1)
    g.sync.wait_ge(sem.cp, 1)
    g.sync.dma_start(T.y[:], T.ys[:]).then_inc(sem.stored, 16)

    if sent[0]:
        g.wait_ge(sem.sent, sent[0])
    g.wait_ge(sem.stored, 16)
